import numpy as np
import ml_dtypes


def mxq(x, axis, fmt="e4m3"):
    dtype, down = {"e4m3": (ml_dtypes.float8_e4m3fn, 7), "e5m2": (ml_dtypes.float8_e5m2, 14)}[fmt]
    v = np.moveaxis(np.asarray(x, np.float32).astype(ml_dtypes.bfloat16).astype(np.float64), axis, -1)
    blocks = v.reshape(v.shape[:-1] + (-1, 32))
    amax = np.abs(blocks).max(-1, keepdims=True)
    byte = np.maximum(np.where(amax > 0, np.frexp(amax)[1] - 1 + 127, 0) - down, 1)
    scale = np.exp2(byte - 127.0)
    codes = (blocks / scale).astype(np.float32).astype(dtype).astype(np.float64)
    return np.moveaxis((codes * scale).reshape(v.shape), -1, axis)


WIDE = False


def mx_kscale(k):
    if not WIDE:
        return np.ones(k)
    levels = np.array([30, -30])
    if k % 512:
        return np.exp2(np.random.permutation(np.resize(levels, k // 32))).repeat(32)
    a = np.empty((k // 512, 16))
    for p in range(k // 512):
        a[p, :8] = np.random.permutation(np.resize(levels, 8))
        for g in range(8):
            far = levels[np.abs(levels - a[p, g]) >= 10]
            a[p, g + 8] = far[np.random.randint(len(far))]
    return np.exp2(a.ravel()).repeat(32)


BF16 = ml_dtypes.bfloat16


def bf(x):
    return np.asarray(x, np.float32).astype(BF16)


def f64(x):
    return np.asarray(x).astype(np.float64)


E2M1 = np.array([0.0, 0.5, 1.0, 1.5, 2.0, 3.0, 4.0, 6.0, -0.0, -0.5, -1.0, -1.5, -2.0, -3.0, -4.0, -6.0])


def pack_weight(w, fmt):
    k, n = w.shape
    w = f64(bf(w)).reshape(k // 32, 32, n)
    amax = np.abs(w).max(1)
    if fmt == "e4m3":
        byte = np.frexp(amax)[1] - 1 + 127 - 7
    else:
        mant, ex = np.frexp(amax / 6.0)
        byte = np.where(mant > 0.5, ex, ex - 1) + 127
    byte = np.clip(np.where(amax > 0, byte, 1), 1, 254)
    scaled = (w * np.exp2(127.0 - byte)[:, None, :]).reshape(k, n).astype(np.float32)
    by_word = np.ascontiguousarray(scaled.reshape(k // 512, 128, 4, n).transpose(0, 1, 3, 2))
    if fmt == "e4m3":
        words = by_word.astype(ml_dtypes.float8_e4m3fn).view(np.uint8)
    else:
        c = by_word.astype(ml_dtypes.float4_e2m1fn).view(np.uint8) & 0xF
        words = c[..., 0::2] | (c[..., 1::2] << 4)
    return np.ascontiguousarray(words), np.ascontiguousarray(byte.astype(np.uint8).reshape(k // 512, 16, n))


def unpack_weight(words, scales, fmt):
    g, p, n, _ = words.shape
    if fmt == "e4m3":
        vals = np.ascontiguousarray(words).view(ml_dtypes.float8_e4m3fn).astype(np.float64)
    else:
        nib = np.empty((g, p, n, 4), np.uint8)
        nib[..., 0::2] = words & 0xF
        nib[..., 1::2] = words >> 4
        vals = E2M1[nib]
    vals = vals * np.repeat(np.exp2(scales.astype(np.float64) - 127.0), 8, axis=1)[..., None]
    return vals.transpose(0, 1, 3, 2).reshape(g * 512, n)
def pack4(w):
    words, scales = pack_weight(w, "e2m1")
    return words.reshape(words.shape[0], 128, -1), scales


def unpack4(words, scales):
    return unpack_weight(words.reshape(words.shape[0], 128, -1, 2), scales, "e2m1")


M, K, N, R = 1024, 1024, 2048, 512

SPREAD = 0.7


def setup_inputs():
    s = mx_kscale(K)
    t = mx_kscale(N)
    x = np.random.standard_normal((M, K)) * s
    z = np.random.standard_normal((K, N)) * SPREAD / np.sqrt(K) / s[:, None]
    z_words, z_scales = pack4(z)
    return {"x": bf(x),
            "z_words": z_words,
            "z_scales": z_scales,
            "c": bf(np.exp(0.3 * np.random.standard_normal(N)) * t),
            "alpha": bf(np.random.standard_normal((N, R)) / np.sqrt(N) / t[:, None]),
            "r": bf(np.exp(0.3 * np.random.standard_normal(M))),
            "b": bf(0.3 * np.random.standard_normal(R))}


def reference(x, z_words, z_scales, c, alpha, r, b):
    z = unpack4(z_words, z_scales)
    dots = mxq(f64(x), 1, "e4m3") @ z
    h = np.exp(dots) * f64(c)
    pred = mxq(h, 1, "e5m2") @ mxq(f64(alpha), 0, "e4m3")
    return pred * f64(r)[:, None] + f64(b)

@@ -1,0 +1,319 @@
+import math
+from contextlib import ExitStack
+
+import concourse.mybir as mybir
+from concourse.masks import make_identity
+
+M, K, N, R = 1024, 1024, 2048, 512
+FLOPS = 2 * M * K * N + 2 * M * N * R
+
+F32 = mybir.dt.float32
+BF16 = mybir.dt.bfloat16
+I32 = mybir.dt.int32
+U32 = mybir.dt.uint32
+U8 = mybir.dt.uint8
+E4M3X4 = mybir.dt.float8_e4m3fn_x4
+E5M2X4 = mybir.dt.float8_e5m2_x4
+E2M1X4 = mybir.dt.float4_e2m1fn_x4
+ALU = mybir.AluOpType
+ACT = mybir.ActivationFunctionType
+
+P = 128
+SLOTS = 4
+K_PASSES = K // 512
+GROUPS = N // 512
+TILES = M // P
+HALF = 4
+SCALAR_COLS = 192
+
+
+def tile_landmark_kernel_ridge_s9_kernel(tc, x, z_words, z_scales, c, alpha, r, b, out):
+    nc = tc.nc
+    with ExitStack() as ctx:
+        keep = ctx.enter_context(tc.tile_pool(name="keep", bufs=1))
+        work = ctx.enter_context(tc.tile_pool(name="work", bufs=3))
+        dots_ps = ctx.enter_context(tc.psum_pool(name="dots_ps", bufs=4))
+        acc_ps = ctx.enter_context(tc.psum_pool(name="acc_ps", bufs=4))
+        ctx.enter_context(tc.manual_schedule())
+
+        def kept(name, count, shape, dtype):
+            return [keep.tile(shape, dtype, name="%s%d" % (name, n), align_bytes=64) for n in range(count)]
+
+        x_raw = kept("x_raw", TILES, [P, K], BF16)
+        x_grouped = kept("x_grouped", TILES, [P, K_PASSES, P * SLOTS], BF16)
+        x_codes = kept("x_codes", 2 * K_PASSES, [P, 512], U32)
+        x_scales = kept("x_scales", 2 * K_PASSES, [P, 512], U8)
+        z_raw = kept("z_raw", GROUPS, [P, K_PASSES, 256], I32)
+        z_codes = kept("z_codes", GROUPS, [P, K_PASSES * SLOTS * 256], U8)
+        a_raw = kept("a_raw", GROUPS, [P, SLOTS, R], BF16)
+        a_signed = kept("a_signed", GROUPS, [P, SLOTS, R], BF16)
+        a_grouped = kept("a_grouped", GROUPS, [P, R, SLOTS], BF16)
+        a_codes = kept("a_codes", GROUPS, [P, R], U32)
+        a_scales = kept("a_scales", GROUPS, [P, R], U8)
+        h_codes = kept("h_codes", 2 * GROUPS, [P, 512], U32)
+        h_scales = kept("h_scales", 2 * GROUPS, [P, 512], U8)
+        y_sb = kept("y_sb", TILES, [P, R], F32)
+        zs_groups = (1, GROUPS - 1)
+        zs_raw = [keep.tile([P, K_PASSES, P * n], I32, name="zs_raw%d" % n, align_bytes=64) for n in zs_groups]
+        zs = [keep.tile([P, K_PASSES * 512 * n], U8, name="zs%d" % n, align_bytes=64) for n in zs_groups]
+        ident = keep.tile([P, P], F32)
+        c_raw = keep.tile([P, GROUPS, 16], BF16)
+        r_sb = keep.tile([P, TILES], BF16)
+        b_sb = keep.tile([P, R], BF16)
+        c_f32 = keep.tile([P, GROUPS, SLOTS], F32)
+        c_expo = keep.tile([P, 16], I32)
+        c_mant = keep.tile([P, 16], I32)
+        c_sign = keep.tile([P, 16], I32)
+        ln_expo = keep.tile([P, 16], F32)
+        zero_cap = keep.tile([P, 16], F32)
+        ln_capped = keep.tile([P, 16], F32)
+        ln_mant = keep.tile([P, 16], F32)
+        ln_c = keep.tile([P, 16], F32)
+        warm_in = keep.tile([P, 1], F32)
+        warm_ln = keep.tile([P, 1], F32)
+        warm_exp = keep.tile([P, 1], F32)
+
+        x_rows = x.rearrange("(m i) k -> i m k", i=TILES)
+        y_rows = out.rearrange("(m i) n -> i m n", i=TILES)
+        z_view = z_words.bitcast(I32).rearrange("g p (G w) -> G p g w", G=GROUPS)
+        a_view = alpha.rearrange("(G a t e) w -> G e a t w", G=GROUPS, t=SLOTS, e=4)
+        c_view = c.rearrange("(G a j) -> a G j", G=GROUPS, j=16)
+        zs_view = z_scales.bitcast(I32).rearrange("g q w -> q g w")
+
+        def load_x(i):
+            nc.sync.dma_start(out=x_raw[i][:], in_=x_rows[i])
+
+        def load_z(G):
+            nc.sync.dma_start(out=z_raw[G][:], in_=z_view[G])
+
+        def load_alpha(G):
+            for e in range(4):
+                nc.sync.dma_start(out=a_raw[G][e:P:4, :, :], in_=a_view[G, e])
+
+        def load_z_scales(part, queue):
+            words = slice(P * part, P * (part + zs_groups[part]))
+            for Q in range(4):
+                queue.dma_start(out=zs_raw[part][32 * Q : 32 * Q + 4, :, :], in_=zs_view[4 * Q : 4 * Q + 4, :, words])
+
+        nc.vector.memset(warm_in[:], 1.0)
+        nc.vector.memset(zs_raw[0][:], 0)
+        nc.vector.memset(zs_raw[1][:], 0)
+        make_identity(nc, ident[:])
+        for e in range(4):
+            nc.scalar.dma_start(out=c_raw[e:P:4, :, 0:13], in_=c_view[:, :, e : e + 13])
+        for i in range(HALF):
+            load_x(i)
+        nc.scalar.activation(out=warm_ln[:], in_=warm_in[:], func=ACT.Ln)
+        load_z_scales(0, nc.scalar)
+        load_z(0)
+        load_alpha(0)
+        load_z_scales(1, nc.sync)
+        load_z(1)
+        load_z(2)
+        for i in range(HALF, TILES):
+            load_x(i)
+        load_z(3)
+        for G in range(1, GROUPS):
+            load_alpha(G)
+        nc.sync.dma_start(out=r_sb[:], in_=r.rearrange("(m i) -> m i", i=TILES))
+        nc.sync.dma_start(out=b_sb[:], in_=b.partition_broadcast(P))
+
+        nc.vector.tensor_copy(out=c_f32[:], in_=c_raw[:, :, 0:13:4])
+        c_bits = c_f32[:].rearrange("p G t -> p (G t)").bitcast(I32)
+        nc.vector.tensor_scalar(out=c_mant[:], in0=c_bits, scalar1=0x007FFFFF, scalar2=0x3F800000,
+                                op0=ALU.bitwise_and, op1=ALU.bitwise_or)
+        nc.vector.tensor_scalar(out=c_expo[:], in0=c_bits, scalar1=23, scalar2=0xFF,
+                                op0=ALU.logical_shift_right, op1=ALU.bitwise_and)
+        nc.vector.tensor_scalar(out=c_sign[:], in0=c_bits, scalar1=-0x80000000, scalar2=0x3F800000,
+                                op0=ALU.bitwise_and, op1=ALU.bitwise_or)
+        nc.scalar.activation(out=ln_mant[:], in_=c_mant[:].bitcast(F32), func=ACT.Ln)
+        nc.scalar.activation(out=warm_exp[:], in_=warm_ln[:], func=ACT.Exp)
+        nc.vector.tensor_scalar(out=ln_expo[:], in0=c_expo[:], scalar1=-127.0, scalar2=math.log(2.0),
+                                op0=ALU.add, op1=ALU.mult)
+        nc.vector.tensor_scalar(out=zero_cap[:], in0=c_expo[:], scalar1=-0.5, scalar2=2.0**100,
+                                op0=ALU.add, op1=ALU.mult)
+        nc.vector.tensor_tensor(out=ln_capped[:], in0=ln_expo[:], in1=zero_cap[:], op=ALU.min)
+        sign = c_sign[:].bitcast(F32)
+
+        def transpose_x(i, engine):
+            words = x_raw[i][:].bitcast(F32)
+            bank = acc_ps.tile([P, 2 * K_PASSES, P], F32, name="acc")
+            for g in range(K_PASSES):
+                for u in range(2):
+                    nc.tensor.transpose(bank[:, 2 * g + u, :], words[:, 256 * g + u : 256 * (g + 1) : 2], ident[:])
+            dst = x_grouped[i][:].bitcast(F32).rearrange("p g (m u) -> p g m u", u=2)
+            src = bank[:].rearrange("p (g u) m -> p g m u", u=2)
+            if engine == "vector":
+                nc.vector.tensor_copy(out=dst, in_=src)
+            else:
+                nc.scalar.copy(out=dst, in_=src)
+
+        def quantize_x(i):
+            cols = slice(P * (i % HALF), P * (i % HALF + 1))
+            for g in range(K_PASSES):
+                n = K_PASSES * (i // HALF) + g
+                nc.vector.quantize_mx(out=x_codes[n][:, cols].bitcast(E4M3X4), scales=x_scales[n][:, cols],
+                                      in_=x_grouped[i][:, g, :])
+
+        def sort_z(G):
+            nc.vector.tensor_copy(
+                out=z_codes[G][:].bitcast(I32).rearrange("p (g t a w) -> p g t a w", g=K_PASSES, t=SLOTS, w=2),
+                in_=z_raw[G][:].rearrange("p g (a t w) -> p g t a w", t=SLOTS, w=2))
+
+        def sort_z_scales(part):
+            nc.vector.tensor_copy(
+                out=zs[part][:].bitcast(I32).rearrange("p (n t s a) -> p n s t a", t=SLOTS, s=8, a=4),
+                in_=zs_raw[part][:].rearrange("p g (G s a t) -> p (g G) s t a", s=8, a=4, t=SLOTS))
+
+        def interleave(engine, dst, src, lo, hi):
+            d = dst[:, lo:hi, :].rearrange("p (s i) t -> p s t i", i=4)
+            s = src[:, :, lo:hi].rearrange("p t (s i) -> p s t i", i=4)
+            if engine == "vector":
+                nc.vector.tensor_copy(out=d, in_=s)
+            else:
+                nc.scalar.copy(out=d, in_=s)
+
+        def sign_alpha(G):
+            for t in range(SLOTS):
+                n = SLOTS * G + t
+                nc.vector.tensor_scalar(out=a_signed[G][:, t, :], in0=a_raw[G][:, t, :], scalar1=sign[:, n : n + 1],
+                                        scalar2=None, op0=ALU.mult)
+
+        def quantize_alpha(G):
+            nc.vector.quantize_mx(out=a_codes[G][:].bitcast(E4M3X4), scales=a_scales[G][:],
+                                  in_=a_grouped[G][:].rearrange("p n t -> p (n t)"))
+
+        h_slots = {}
+        h_grouped = {}
+
+        def stage1(unit):
+            half, G = divmod(unit, GROUPS)
+            h_slots[unit] = work.tile([P, SLOTS, 512], BF16, name="h_slots", align_bytes=64)
+            for t in range(SLOTS):
+                bank = dots_ps.tile([P, 512], F32, name="dots")
+                for g in range(K_PASSES):
+                    w0 = 256 * (SLOTS * g + t)
+                    part = min(G, 1)
+                    s0 = 512 * (zs_groups[part] * g + G - part) + P * t
+                    n = K_PASSES * half + g
+                    nc.tensor.matmul_mx(out=bank[:], lhsT=z_codes[G][:, w0 : w0 + 256].bitcast(E2M1X4),
+                                        lhsT_scale=zs[part][:, s0 : s0 + P], rhs=x_codes[n][:].bitcast(E4M3X4),
+                                        rhs_scale=x_scales[n][:], start=(g == 0), stop=(g == K_PASSES - 1))
+                n = SLOTS * G + t
+                nc.scalar.activation(out=h_slots[unit][:, t, :], in_=bank[:], func=ACT.Exp, bias=ln_c[:, n : n + 1])
+
+        def group_h(unit, engine="vector", lo=0, hi=512):
+            if unit not in h_grouped:
+                h_grouped[unit] = work.tile([P, 512, SLOTS], BF16, name="h_grouped", align_bytes=64)
+            interleave(engine, h_grouped[unit], h_slots[unit], lo, hi)
+
+        def quantize_h(unit, lo=0, hi=512):
+            nc.vector.quantize_mx(out=h_codes[unit][:, lo:hi].bitcast(E5M2X4), scales=h_scales[unit][:, lo:hi],
+                                  in_=h_grouped[unit][:, lo:hi, :].rearrange("p n t -> p (n t)"))
+
+        acc = {}
+
+        def stage2(i, groups):
+            cols = slice(P * (i % HALF), P * (i % HALF + 1))
+            for G in groups:
+                if G == 0:
+                    acc[i] = acc_ps.tile([P, R], F32, name="acc")
+                unit = GROUPS * (i // HALF) + G
+                nc.tensor.matmul_mx(out=acc[i][:], lhsT=h_codes[unit][:, cols].bitcast(E5M2X4),
+                                    lhsT_scale=h_scales[unit][:, cols], rhs=a_codes[G][:].bitcast(E4M3X4),
+                                    rhs_scale=a_scales[G][:], start=(G == 0), stop=(G == GROUPS - 1))
+
+        def stage2_first_half(G):
+            for i in range(HALF):
+                stage2(i, [G])
+
+        def finish(i):
+            nc.vector.scalar_tensor_tensor(out=y_sb[i][:], in0=acc[i][:], scalar=r_sb[:, i : i + 1], in1=b_sb[:],
+                                           op0=ALU.mult, op1=ALU.add)
+            nc.sync.dma_start(out=y_rows[i], in_=y_sb[i][:])
+
+        split = R - SCALAR_COLS
+
+        transpose_x(0, "vector")
+        transpose_x(1, "vector")
+        quantize_x(0)
+        nc.vector.tensor_tensor(out=ln_c[:], in0=ln_mant[:], in1=ln_capped[:], op=ALU.add)
+        transpose_x(2, "vector")
+        quantize_x(1)
+        transpose_x(3, "vector")
+        quantize_x(2)
+        sort_z_scales(0)
+        sort_z(0)
+        quantize_x(3)
+
+        stage1(0)
+        sign_alpha(0)
+        sort_z_scales(1)
+        sort_z(1)
+        interleave("vector", a_grouped[0], a_signed[0], 0, R)
+        sort_z(2)
+        quantize_alpha(0)
+        stage1(1)
+        group_h(0)
+        sort_z(3)
+        quantize_h(0)
+        for i in range(HALF, TILES):
+            transpose_x(i, "scalar")
+        group_h(1)
+        sign_alpha(1)
+        quantize_h(1)
+        stage1(2)
+        interleave("vector", a_grouped[1], a_signed[1], 0, split)
+        interleave("scalar", a_grouped[1], a_signed[1], split, R)
+        for i in range(HALF, TILES):
+            quantize_x(i)
+        stage2_first_half(0)
+        group_h(2)
+        sign_alpha(2)
+        quantize_h(2)
+        quantize_alpha(1)
+        stage1(3)
+        interleave("vector", a_grouped[2], a_signed[2], 0, split)
+        interleave("scalar", a_grouped[2], a_signed[2], split, R)
+        stage2_first_half(1)
+        sign_alpha(3)
+        group_h(3)
+        quantize_alpha(2)
+        quantize_h(3)
+        stage1(4)
+        interleave("vector", a_grouped[3], a_signed[3], 0, split)
+        interleave("scalar", a_grouped[3], a_signed[3], split, R)
+        stage2_first_half(2)
+        group_h(4)
+        quantize_alpha(3)
+        quantize_h(4)
+        stage1(5)
+        stage2_first_half(3)
+        group_h(5)
+        finish(0)
+        quantize_h(5)
+        stage1(6)
+        finish(1)
+        finish(2)
+        group_h(6)
+        finish(3)
+        quantize_h(6)
+        stage1(7)
+        group_h(7, "vector", 0, 128)
+        group_h(7, "scalar", 256, 384)
+        group_h(7, "vector", 128, 256)
+        group_h(7, "scalar", 384, 512)
+        quantize_h(7, 0, 128)
+        quantize_h(7, 128, 256)
+        quantize_h(7, 256, 384)
+        quantize_h(7, 384, 512)
+        stage2(4, range(3))
+        stage2(5, range(3))
+        stage2(4, [3])
+        stage2(5, [3])
+        finish(4)
+        finish(5)
+        stage2(6, range(4))
+        finish(6)
+        stage2(7, range(4))
+        finish(7)

@@ -106,15 +106,17 @@ def tile_landmark_kernel_ridge_s9_kernel(tc, x, z_words, z_scales, c, alpha, r, 
         nc.scalar.activation(out=warm_ln[:], in_=warm_in[:], func=ACT.Ln)
         load_z_scales(0, nc.scalar)
         load_z(0)
+        load_x(4)
         load_alpha(0)
         load_z_scales(1, nc.sync)
         load_z(1)
-        load_z(2)
-        for i in range(HALF, TILES):
+        for i in range(HALF + 1, TILES):
             load_x(i)
+        load_z(2)
+        load_alpha(1)
         load_z(3)
-        for G in range(1, GROUPS):
-            load_alpha(G)
+        load_alpha(2)
+        load_alpha(3)
         nc.sync.dma_start(out=r_sb[:], in_=r.rearrange("(m i) -> m i", i=TILES))
         nc.sync.dma_start(out=b_sb[:], in_=b.partition_broadcast(P))
 
@@ -186,7 +188,7 @@ def tile_landmark_kernel_ridge_s9_kernel(tc, x, z_words, z_scales, c, alpha, r, 
         h_slots = {}
         h_grouped = {}
 
-        def stage1(unit):
+        def stage1(unit, share_of=None):
             half, G = divmod(unit, GROUPS)
             h_slots[unit] = work.tile([P, SLOTS, 512], BF16, name="h_slots", align_bytes=64)
             for t in range(SLOTS):
@@ -201,6 +203,8 @@ def tile_landmark_kernel_ridge_s9_kernel(tc, x, z_words, z_scales, c, alpha, r, 
                                         rhs_scale=x_scales[n][:], start=(g == 0), stop=(g == K_PASSES - 1))
                 n = SLOTS * G + t
                 nc.scalar.activation(out=h_slots[unit][:, t, :], in_=bank[:], func=ACT.Exp, bias=ln_c[:, n : n + 1])
+                if t == 0 and share_of is not None:
+                    group_h(share_of, "scalar", split, 512)
 
         def group_h(unit, engine="vector", lo=0, hi=512):
             if unit not in h_grouped:
@@ -227,78 +231,78 @@ def tile_landmark_kernel_ridge_s9_kernel(tc, x, z_words, z_scales, c, alpha, r, 
             for i in range(HALF):
                 stage2(i, [G])
 
-        def finish(i):
-            nc.vector.scalar_tensor_tensor(out=y_sb[i][:], in0=acc[i][:], scalar=r_sb[:, i : i + 1], in1=b_sb[:],
-                                           op0=ALU.mult, op1=ALU.add)
-            nc.sync.dma_start(out=y_rows[i], in_=y_sb[i][:])
+        def finish(i, lo=0, hi=R):
+            nc.vector.scalar_tensor_tensor(out=y_sb[i][:, lo:hi], in0=acc[i][:, lo:hi], scalar=r_sb[:, i : i + 1],
+                                           in1=b_sb[:, lo:hi], op0=ALU.mult, op1=ALU.add)
+            nc.sync.dma_start(out=y_rows[i][:, lo:hi], in_=y_sb[i][:, lo:hi])
 
-        split = R - SCALAR_COLS
+        split = 512 - SCALAR_COLS
+
+        def group_alpha(G):
+            interleave("vector", a_grouped[G], a_signed[G], 0, R)
 
         transpose_x(0, "vector")
         transpose_x(1, "vector")
         quantize_x(0)
         nc.vector.tensor_tensor(out=ln_c[:], in0=ln_mant[:], in1=ln_capped[:], op=ALU.add)
-        transpose_x(2, "vector")
+        transpose_x(2, "scalar")
+        transpose_x(3, "scalar")
         quantize_x(1)
-        transpose_x(3, "vector")
-        quantize_x(2)
         sort_z_scales(0)
         sort_z(0)
+        quantize_x(2)
         quantize_x(3)
+        transpose_x(4, "scalar")
 
         stage1(0)
         sign_alpha(0)
         sort_z_scales(1)
         sort_z(1)
-        interleave("vector", a_grouped[0], a_signed[0], 0, R)
-        sort_z(2)
+        group_alpha(0)
+        quantize_x(4)
         quantize_alpha(0)
         stage1(1)
         group_h(0)
-        sort_z(3)
+        sort_z(2)
         quantize_h(0)
-        for i in range(HALF, TILES):
+        for i in range(HALF + 1, TILES):
             transpose_x(i, "scalar")
-        group_h(1)
         sign_alpha(1)
-        quantize_h(1)
-        stage1(2)
-        interleave("vector", a_grouped[1], a_signed[1], 0, split)
-        interleave("scalar", a_grouped[1], a_signed[1], split, R)
-        for i in range(HALF, TILES):
-            quantize_x(i)
-        stage2_first_half(0)
-        group_h(2)
-        sign_alpha(2)
-        quantize_h(2)
+        sort_z(3)
+        group_alpha(1)
+        group_h(1, "vector", 0, split)
         quantize_alpha(1)
-        stage1(3)
-        interleave("vector", a_grouped[2], a_signed[2], 0, split)
-        interleave("scalar", a_grouped[2], a_signed[2], split, R)
+        stage1(2, 1)
+        stage2_first_half(0)
+        sign_alpha(2)
+        quantize_h(1)
+        for i in range(HALF + 1, TILES):
+            quantize_x(i)
+        group_alpha(2)
+        group_h(2, "vector", 0, split)
+        quantize_alpha(2)
+        stage1(3, 2)
         stage2_first_half(1)
         sign_alpha(3)
-        group_h(3)
-        quantize_alpha(2)
-        quantize_h(3)
-        stage1(4)
-        interleave("vector", a_grouped[3], a_signed[3], 0, split)
-        interleave("scalar", a_grouped[3], a_signed[3], split, R)
-        stage2_first_half(2)
-        group_h(4)
+        quantize_h(2)
+        group_alpha(3)
+        group_h(3, "vector", 0, split)
         quantize_alpha(3)
-        quantize_h(4)
-        stage1(5)
+        stage1(4, 3)
+        stage2_first_half(2)
+        quantize_h(3)
+        group_h(4, "vector", 0, split)
+        stage1(5, 4)
         stage2_first_half(3)
-        group_h(5)
-        finish(0)
+        quantize_h(4)
+        group_h(5, "vector", 0, split)
+        for i in range(HALF):
+            finish(i)
+        stage1(6, 5)
         quantize_h(5)
-        stage1(6)
-        finish(1)
-        finish(2)
         group_h(6)
-        finish(3)
-        quantize_h(6)
         stage1(7)
+        quantize_h(6)
         group_h(7, "vector", 0, 128)
         group_h(7, "scalar", 256, 384)
         group_h(7, "vector", 128, 256)
@@ -307,13 +311,12 @@ def tile_landmark_kernel_ridge_s9_kernel(tc, x, z_words, z_scales, c, alpha, r, 
         quantize_h(7, 128, 256)
         quantize_h(7, 256, 384)
         quantize_h(7, 384, 512)
-        stage2(4, range(3))
-        stage2(5, range(3))
-        stage2(4, [3])
-        stage2(5, [3])
-        finish(4)
-        finish(5)
-        stage2(6, range(4))
-        finish(6)
+        for G in (0, 1, 2):
+            for i in (4, 5, 6):
+                stage2(i, [G])
+        for i in (4, 5, 6):
+            stage2(i, [3])
+            finish(i)
         stage2(7, range(4))
-        finish(7)
+        finish(7, 0, R // 2)
+        finish(7, R // 2, R)

@@ -1,4 +1,3 @@
-import math
 from contextlib import ExitStack
 
 import concourse.mybir as mybir
@@ -24,7 +23,7 @@ K_PASSES = K // 512
 GROUPS = N // 512
 TILES = M // P
 HALF = 4
-SCALAR_COLS = 192
+SCALAR_COLS = 176
 
 
 def tile_landmark_kernel_ridge_s9_kernel(tc, x, z_words, z_scales, c, alpha, r, b, out):
@@ -39,8 +38,8 @@ def tile_landmark_kernel_ridge_s9_kernel(tc, x, z_words, z_scales, c, alpha, r, 
         def kept(name, count, shape, dtype):
             return [keep.tile(shape, dtype, name="%s%d" % (name, n), align_bytes=64) for n in range(count)]
 
-        x_raw = kept("x_raw", TILES, [P, K], BF16)
-        x_grouped = kept("x_grouped", TILES, [P, K_PASSES, P * SLOTS], BF16)
+        x_raw = kept("x_raw", TILES, [P, 2, 512], BF16)
+        x_grouped = kept("x_grouped", TILES, [P, 2 * P * SLOTS], BF16)
         x_codes = kept("x_codes", 2 * K_PASSES, [P, 512], U32)
         x_scales = kept("x_scales", 2 * K_PASSES, [P, 512], U8)
         z_raw = kept("z_raw", GROUPS, [P, K_PASSES, 256], I32)
@@ -69,11 +68,10 @@ def tile_landmark_kernel_ridge_s9_kernel(tc, x, z_words, z_scales, c, alpha, r, 
         ln_capped = keep.tile([P, 16], F32)
         ln_mant = keep.tile([P, 16], F32)
         ln_c = keep.tile([P, 16], F32)
-        warm_in = keep.tile([P, 1], F32)
-        warm_ln = keep.tile([P, 1], F32)
-        warm_exp = keep.tile([P, 1], F32)
+        two = keep.tile([P, 1], F32)
+        ln_two = keep.tile([P, 1], F32)
 
-        x_rows = x.rearrange("(m i) k -> i m k", i=TILES)
+        x_view = x.rearrange("(m h q i) (g k) -> h g q m i k", h=2, q=2, i=2, g=K_PASSES)
         y_rows = out.rearrange("(m i) n -> i m n", i=TILES)
         z_view = z_words.bitcast(I32).rearrange("g p (G w) -> G p g w", G=GROUPS)
         a_view = alpha.rearrange("(G a t e) w -> G e a t w", G=GROUPS, t=SLOTS, e=4)
@@ -81,7 +79,7 @@ def tile_landmark_kernel_ridge_s9_kernel(tc, x, z_words, z_scales, c, alpha, r, 
         zs_view = z_scales.bitcast(I32).rearrange("g q w -> q g w")
 
         def load_x(i):
-            nc.sync.dma_start(out=x_raw[i][:], in_=x_rows[i])
+            nc.sync.dma_start(out=x_raw[i][:], in_=x_view[i // 4, i // 2 % 2, i % 2])
 
         def load_z(G):
             nc.sync.dma_start(out=z_raw[G][:], in_=z_view[G])
@@ -95,67 +93,67 @@ def tile_landmark_kernel_ridge_s9_kernel(tc, x, z_words, z_scales, c, alpha, r, 
             for Q in range(4):
                 queue.dma_start(out=zs_raw[part][32 * Q : 32 * Q + 4, :, :], in_=zs_view[4 * Q : 4 * Q + 4, :, words])
 
-        nc.vector.memset(warm_in[:], 1.0)
+        nc.vector.memset(two[:], 2.0)
         nc.vector.memset(zs_raw[0][:], 0)
         nc.vector.memset(zs_raw[1][:], 0)
         make_identity(nc, ident[:])
         for e in range(4):
             nc.scalar.dma_start(out=c_raw[e:P:4, :, 0:13], in_=c_view[:, :, e : e + 13])
+        nc.scalar.activation(out=ln_two[:], in_=two[:], func=ACT.Ln)
         for i in range(HALF):
             load_x(i)
-        nc.scalar.activation(out=warm_ln[:], in_=warm_in[:], func=ACT.Ln)
-        load_z_scales(0, nc.scalar)
+        load_z_scales(0, nc.sync)
         load_z(0)
-        load_x(4)
         load_alpha(0)
         load_z_scales(1, nc.sync)
         load_z(1)
-        for i in range(HALF + 1, TILES):
-            load_x(i)
         load_z(2)
         load_alpha(1)
+        for i in range(HALF, TILES):
+            load_x(i)
         load_z(3)
         load_alpha(2)
         load_alpha(3)
         nc.sync.dma_start(out=r_sb[:], in_=r.rearrange("(m i) -> m i", i=TILES))
         nc.sync.dma_start(out=b_sb[:], in_=b.partition_broadcast(P))
 
-        nc.vector.tensor_copy(out=c_f32[:], in_=c_raw[:, :, 0:13:4])
         c_bits = c_f32[:].rearrange("p G t -> p (G t)").bitcast(I32)
-        nc.vector.tensor_scalar(out=c_mant[:], in0=c_bits, scalar1=0x007FFFFF, scalar2=0x3F800000,
-                                op0=ALU.bitwise_and, op1=ALU.bitwise_or)
-        nc.vector.tensor_scalar(out=c_expo[:], in0=c_bits, scalar1=23, scalar2=0xFF,
-                                op0=ALU.logical_shift_right, op1=ALU.bitwise_and)
-        nc.vector.tensor_scalar(out=c_sign[:], in0=c_bits, scalar1=-0x80000000, scalar2=0x3F800000,
-                                op0=ALU.bitwise_and, op1=ALU.bitwise_or)
-        nc.scalar.activation(out=ln_mant[:], in_=c_mant[:].bitcast(F32), func=ACT.Ln)
-        nc.scalar.activation(out=warm_exp[:], in_=warm_ln[:], func=ACT.Exp)
-        nc.vector.tensor_scalar(out=ln_expo[:], in0=c_expo[:], scalar1=-127.0, scalar2=math.log(2.0),
-                                op0=ALU.add, op1=ALU.mult)
-        nc.vector.tensor_scalar(out=zero_cap[:], in0=c_expo[:], scalar1=-0.5, scalar2=2.0**100,
-                                op0=ALU.add, op1=ALU.mult)
-        nc.vector.tensor_tensor(out=ln_capped[:], in0=ln_expo[:], in1=zero_cap[:], op=ALU.min)
         sign = c_sign[:].bitcast(F32)
 
+        def widen_c():
+            nc.vector.tensor_copy(out=c_f32[:], in_=c_raw[:, :, 0:13:4])
+
+        def split_c():
+            nc.vector.tensor_scalar(out=c_mant[:], in0=c_bits, scalar1=0x007FFFFF, scalar2=0x3F800000,
+                                    op0=ALU.bitwise_and, op1=ALU.bitwise_or)
+            nc.vector.tensor_scalar(out=c_expo[:], in0=c_bits, scalar1=23, scalar2=0xFF,
+                                    op0=ALU.logical_shift_right, op1=ALU.bitwise_and)
+            nc.vector.tensor_scalar(out=c_sign[:], in0=c_bits, scalar1=-0x80000000, scalar2=0x3F800000,
+                                    op0=ALU.bitwise_and, op1=ALU.bitwise_or)
+
+        def ln_exponent():
+            nc.vector.tensor_scalar(out=ln_expo[:], in0=c_expo[:], scalar1=-127.0, scalar2=ln_two[:],
+                                    op0=ALU.add, op1=ALU.mult)
+            nc.vector.tensor_scalar(out=zero_cap[:], in0=c_expo[:], scalar1=-0.5, scalar2=2.0**100,
+                                    op0=ALU.add, op1=ALU.mult)
+
         def transpose_x(i, engine):
-            words = x_raw[i][:].bitcast(F32)
-            bank = acc_ps.tile([P, 2 * K_PASSES, P], F32, name="acc")
-            for g in range(K_PASSES):
+            bank = acc_ps.tile([P, 4, P], F32, name="acc")
+            for j in range(2):
+                words = x_raw[i][:, j, :].bitcast(F32)
                 for u in range(2):
-                    nc.tensor.transpose(bank[:, 2 * g + u, :], words[:, 256 * g + u : 256 * (g + 1) : 2], ident[:])
-            dst = x_grouped[i][:].bitcast(F32).rearrange("p g (m u) -> p g m u", u=2)
-            src = bank[:].rearrange("p (g u) m -> p g m u", u=2)
+                    nc.tensor.transpose(bank[:, 2 * j + u, :], words[:, u:256:2], ident[:])
+            dst = x_grouped[i][:].bitcast(F32).rearrange("p (j m u) -> p j m u", j=2, u=2)
+            src = bank[:].rearrange("p (j u) m -> p j m u", u=2)
             if engine == "vector":
                 nc.vector.tensor_copy(out=dst, in_=src)
             else:
                 nc.scalar.copy(out=dst, in_=src)
 
         def quantize_x(i):
-            cols = slice(P * (i % HALF), P * (i % HALF + 1))
-            for g in range(K_PASSES):
-                n = K_PASSES * (i // HALF) + g
-                nc.vector.quantize_mx(out=x_codes[n][:, cols].bitcast(E4M3X4), scales=x_scales[n][:, cols],
-                                      in_=x_grouped[i][:, g, :])
+            cols = slice(256 * (i % 2), 256 * (i % 2 + 1))
+            nc.vector.quantize_mx(out=x_codes[i // 2][:, cols].bitcast(E4M3X4), scales=x_scales[i // 2][:, cols],
+                                  in_=x_grouped[i][:])
 
         def sort_z(G):
             nc.vector.tensor_copy(
@@ -191,20 +189,24 @@ def tile_landmark_kernel_ridge_s9_kernel(tc, x, z_words, z_scales, c, alpha, r, 
         def stage1(unit, share_of=None):
             half, G = divmod(unit, GROUPS)
             h_slots[unit] = work.tile([P, SLOTS, 512], BF16, name="h_slots", align_bytes=64)
-            for t in range(SLOTS):
-                bank = dots_ps.tile([P, 512], F32, name="dots")
-                for g in range(K_PASSES):
-                    w0 = 256 * (SLOTS * g + t)
-                    part = min(G, 1)
-                    s0 = 512 * (zs_groups[part] * g + G - part) + P * t
-                    n = K_PASSES * half + g
-                    nc.tensor.matmul_mx(out=bank[:], lhsT=z_codes[G][:, w0 : w0 + 256].bitcast(E2M1X4),
-                                        lhsT_scale=zs[part][:, s0 : s0 + P], rhs=x_codes[n][:].bitcast(E4M3X4),
-                                        rhs_scale=x_scales[n][:], start=(g == 0), stop=(g == K_PASSES - 1))
-                n = SLOTS * G + t
-                nc.scalar.activation(out=h_slots[unit][:, t, :], in_=bank[:], func=ACT.Exp, bias=ln_c[:, n : n + 1])
-                if t == 0 and share_of is not None:
-                    group_h(share_of, "scalar", split, 512)
+            banks = [dots_ps.tile([P, 512], F32, name="dots") for t in range(SLOTS)]
+            order = [(t, g) for t in range(SLOTS) for g in range(K_PASSES)]
+            if unit == 0:
+                order = [(t, g) for g in range(K_PASSES) for t in range(SLOTS)]
+            for t, g in order:
+                w0 = 256 * (SLOTS * g + t)
+                part = min(G, 1)
+                s0 = 512 * (zs_groups[part] * g + G - part) + P * t
+                n = K_PASSES * half + g
+                nc.tensor.matmul_mx(out=banks[t][:], lhsT=z_codes[G][:, w0 : w0 + 256].bitcast(E2M1X4),
+                                    lhsT_scale=zs[part][:, s0 : s0 + P], rhs=x_codes[n][:].bitcast(E4M3X4),
+                                    rhs_scale=x_scales[n][:], start=(g == 0), stop=(g == K_PASSES - 1))
+                if g == K_PASSES - 1:
+                    n = SLOTS * G + t
+                    nc.scalar.activation(out=h_slots[unit][:, t, :], in_=banks[t][:], func=ACT.Exp,
+                                         bias=ln_c[:, n : n + 1])
+                    if t == 0 and share_of is not None:
+                        group_h(share_of, "scalar", split, 512)
 
         def group_h(unit, engine="vector", lo=0, hi=512):
             if unit not in h_grouped:
@@ -238,45 +240,47 @@ def tile_landmark_kernel_ridge_s9_kernel(tc, x, z_words, z_scales, c, alpha, r, 
 
         split = 512 - SCALAR_COLS
 
-        def group_alpha(G):
-            interleave("vector", a_grouped[G], a_signed[G], 0, R)
+        def group_alpha(G, engine="vector", lo=0, hi=R):
+            interleave(engine, a_grouped[G], a_signed[G], lo, hi)
 
         transpose_x(0, "vector")
-        transpose_x(1, "vector")
-        quantize_x(0)
-        nc.vector.tensor_tensor(out=ln_c[:], in0=ln_mant[:], in1=ln_capped[:], op=ALU.add)
+        transpose_x(1, "scalar")
         transpose_x(2, "scalar")
         transpose_x(3, "scalar")
+        widen_c()
+        quantize_x(0)
+        split_c()
+        nc.scalar.activation(out=ln_mant[:], in_=c_mant[:].bitcast(F32), func=ACT.Ln)
         quantize_x(1)
         sort_z_scales(0)
+        ln_exponent()
         sort_z(0)
         quantize_x(2)
+        nc.vector.tensor_tensor(out=ln_capped[:], in0=ln_expo[:], in1=zero_cap[:], op=ALU.min)
         quantize_x(3)
-        transpose_x(4, "scalar")
-
-        stage1(0)
+        nc.vector.tensor_tensor(out=ln_c[:], in0=ln_mant[:], in1=ln_capped[:], op=ALU.add)
         sign_alpha(0)
+        stage1(0)
         sort_z_scales(1)
         sort_z(1)
-        group_alpha(0)
-        quantize_x(4)
+        group_alpha(0, "vector", 0, R - 0)
+        sort_z(2)
         quantize_alpha(0)
         stage1(1)
-        group_h(0)
-        sort_z(2)
-        quantize_h(0)
-        for i in range(HALF + 1, TILES):
-            transpose_x(i, "scalar")
         sign_alpha(1)
-        sort_z(3)
+        group_h(0)
+        for i in range(HALF, TILES):
+            transpose_x(i, "scalar")
         group_alpha(1)
+        quantize_h(0)
         group_h(1, "vector", 0, split)
+        sort_z(3)
         quantize_alpha(1)
         stage1(2, 1)
         stage2_first_half(0)
         sign_alpha(2)
         quantize_h(1)
-        for i in range(HALF + 1, TILES):
+        for i in range(HALF, TILES):
             quantize_x(i)
         group_alpha(2)
         group_h(2, "vector", 0, split)
@@ -295,28 +299,35 @@ def tile_landmark_kernel_ridge_s9_kernel(tc, x, z_words, z_scales, c, alpha, r, 
         stage1(5, 4)
         stage2_first_half(3)
         quantize_h(4)
-        group_h(5, "vector", 0, split)
-        for i in range(HALF):
-            finish(i)
-        stage1(6, 5)
+        finish(0)
+        finish(1)
+        group_h(5)
+        finish(2)
+        stage1(6)
+        finish(3)
         quantize_h(5)
-        group_h(6)
+        group_h(6, "vector", 0, 256)
+        group_h(6, "vector", 256, 512)
         stage1(7)
-        quantize_h(6)
+        quantize_h(6, 0, 256)
+        quantize_h(6, 256, 512)
         group_h(7, "vector", 0, 128)
+        group_h(7, "scalar", 128, 256)
         group_h(7, "scalar", 256, 384)
-        group_h(7, "vector", 128, 256)
         group_h(7, "scalar", 384, 512)
         quantize_h(7, 0, 128)
         quantize_h(7, 128, 256)
         quantize_h(7, 256, 384)
-        quantize_h(7, 384, 512)
-        for G in (0, 1, 2):
-            for i in (4, 5, 6):
-                stage2(i, [G])
         for i in (4, 5, 6):
-            stage2(i, [3])
-            finish(i)
+            stage2(i, [0, 1])
+        for G in (2, 3):
+            stage2(4, [G])
+            stage2(5, [G])
+        finish(4)
+        quantize_h(7, 384, 512)
+        finish(5)
+        stage2(6, [2, 3])
+        finish(6)
         stage2(7, range(4))
         finish(7, 0, R // 2)
         finish(7, R // 2, R)

@@ -194,6 +194,9 @@ def tile_landmark_kernel_ridge_s9_kernel(tc, x, z_words, z_scales, c, alpha, r, 
             if unit == 0:
                 order = [(t, g) for g in range(K_PASSES) for t in range(SLOTS)]
             for t, g in order:
+                if unit == 2 and (t, g) == (1, 0):
+                    transpose_x(6, "scalar")
+                    transpose_x(7, "scalar")
                 w0 = 256 * (SLOTS * g + t)
                 part = min(G, 1)
                 s0 = 512 * (zs_groups[part] * g + G - part) + P * t
@@ -269,8 +272,8 @@ def tile_landmark_kernel_ridge_s9_kernel(tc, x, z_words, z_scales, c, alpha, r, 
         stage1(1)
         sign_alpha(1)
         group_h(0)
-        for i in range(HALF, TILES):
-            transpose_x(i, "scalar")
+        transpose_x(4, "scalar")
+        transpose_x(5, "scalar")
         group_alpha(1)
         quantize_h(0)
         group_h(1, "vector", 0, split)

@@ -19,11 +19,18 @@ ACT = mybir.ActivationFunctionType
 
 P = 128
 SLOTS = 4
-K_PASSES = K // 512
-GROUPS = N // 512
+PASS = P * SLOTS
+RUN = 4
+K_PASSES = K // PASS
+GROUPS = N // PASS
 TILES = M // P
-HALF = 4
+HALF_TILES = TILES // 2
+HALF_COLS = HALF_TILES * P
+PIECES = TILES
+C_ROW = SLOTS * RUN
+C_SPAN = C_ROW - RUN + 1
 SCALAR_COLS = 176
+VECTOR_COLS = HALF_COLS - SCALAR_COLS
 
 
 def tile_landmark_kernel_ridge_s9_kernel(tc, x, z_words, z_scales, c, alpha, r, b, out):
@@ -31,86 +38,87 @@ def tile_landmark_kernel_ridge_s9_kernel(tc, x, z_words, z_scales, c, alpha, r, 
     with ExitStack() as ctx:
         keep = ctx.enter_context(tc.tile_pool(name="keep", bufs=1))
         work = ctx.enter_context(tc.tile_pool(name="work", bufs=3))
-        dots_ps = ctx.enter_context(tc.psum_pool(name="dots_ps", bufs=4))
-        acc_ps = ctx.enter_context(tc.psum_pool(name="acc_ps", bufs=4))
+        dots_ps = ctx.enter_context(tc.psum_pool(name="dots_ps", bufs=SLOTS))
+        acc_ps = ctx.enter_context(tc.psum_pool(name="acc_ps", bufs=HALF_TILES))
         ctx.enter_context(tc.manual_schedule())
 
         def kept(name, count, shape, dtype):
             return [keep.tile(shape, dtype, name="%s%d" % (name, n), align_bytes=64) for n in range(count)]
 
-        x_raw = kept("x_raw", TILES, [P, 2, 512], BF16)
-        x_grouped = kept("x_grouped", TILES, [P, 2 * P * SLOTS], BF16)
-        x_codes = kept("x_codes", 2 * K_PASSES, [P, 512], U32)
-        x_scales = kept("x_scales", 2 * K_PASSES, [P, 512], U8)
-        z_raw = kept("z_raw", GROUPS, [P, K_PASSES, 256], I32)
-        z_codes = kept("z_codes", GROUPS, [P, K_PASSES * SLOTS * 256], U8)
+        x_raw = kept("x_raw", PIECES, [P, 2, PASS], BF16)
+        x_grouped = kept("x_grouped", PIECES, [P, 2 * P * SLOTS], BF16)
+        x_codes = kept("x_codes", 2 * K_PASSES, [P, HALF_COLS], U32)
+        x_scales = kept("x_scales", 2 * K_PASSES, [P, HALF_COLS], U8)
+        z_raw = kept("z_raw", GROUPS, [P, K_PASSES, PASS // 2], I32)
+        z_codes = kept("z_codes", GROUPS, [P, K_PASSES * SLOTS * 2 * P], U8)
         a_raw = kept("a_raw", GROUPS, [P, SLOTS, R], BF16)
         a_signed = kept("a_signed", GROUPS, [P, SLOTS, R], BF16)
         a_grouped = kept("a_grouped", GROUPS, [P, R, SLOTS], BF16)
         a_codes = kept("a_codes", GROUPS, [P, R], U32)
         a_scales = kept("a_scales", GROUPS, [P, R], U8)
-        h_codes = kept("h_codes", 2 * GROUPS, [P, 512], U32)
-        h_scales = kept("h_scales", 2 * GROUPS, [P, 512], U8)
+        h_codes = kept("h_codes", 2 * GROUPS, [P, HALF_COLS], U32)
+        h_scales = kept("h_scales", 2 * GROUPS, [P, HALF_COLS], U8)
         y_sb = kept("y_sb", TILES, [P, R], F32)
         zs_groups = (1, GROUPS - 1)
         zs_raw = [keep.tile([P, K_PASSES, P * n], I32, name="zs_raw%d" % n, align_bytes=64) for n in zs_groups]
-        zs = [keep.tile([P, K_PASSES * 512 * n], U8, name="zs%d" % n, align_bytes=64) for n in zs_groups]
+        zs = [keep.tile([P, K_PASSES * PASS * n], U8, name="zs%d" % n, align_bytes=64) for n in zs_groups]
         ident = keep.tile([P, P], F32)
-        c_raw = keep.tile([P, GROUPS, 16], BF16)
+        c_raw = keep.tile([P, GROUPS, C_ROW], BF16)
         r_sb = keep.tile([P, TILES], BF16)
         b_sb = keep.tile([P, R], BF16)
         c_f32 = keep.tile([P, GROUPS, SLOTS], F32)
-        c_expo = keep.tile([P, 16], I32)
-        c_mant = keep.tile([P, 16], I32)
-        c_sign = keep.tile([P, 16], I32)
-        ln_expo = keep.tile([P, 16], F32)
-        zero_cap = keep.tile([P, 16], F32)
-        ln_capped = keep.tile([P, 16], F32)
-        ln_mant = keep.tile([P, 16], F32)
-        ln_c = keep.tile([P, 16], F32)
+        c_expo = keep.tile([P, GROUPS * SLOTS], I32)
+        c_mant = keep.tile([P, GROUPS * SLOTS], I32)
+        c_sign = keep.tile([P, GROUPS * SLOTS], I32)
+        ln_expo = keep.tile([P, GROUPS * SLOTS], F32)
+        zero_cap = keep.tile([P, GROUPS * SLOTS], F32)
+        ln_capped = keep.tile([P, GROUPS * SLOTS], F32)
+        ln_mant = keep.tile([P, GROUPS * SLOTS], F32)
+        ln_c = keep.tile([P, GROUPS * SLOTS], F32)
         two = keep.tile([P, 1], F32)
         ln_two = keep.tile([P, 1], F32)
 
-        x_view = x.rearrange("(m h q i) (g k) -> h g q m i k", h=2, q=2, i=2, g=K_PASSES)
+        x_view = x.rearrange("(m h pair j) (g k) -> h g pair m j k", h=2, pair=2, j=2, g=K_PASSES)
         y_rows = out.rearrange("(m i) n -> i m n", i=TILES)
         z_view = z_words.bitcast(I32).rearrange("g p (G w) -> G p g w", G=GROUPS)
-        a_view = alpha.rearrange("(G a t e) w -> G e a t w", G=GROUPS, t=SLOTS, e=4)
-        c_view = c.rearrange("(G a j) -> a G j", G=GROUPS, j=16)
+        a_view = alpha.rearrange("(G a t e) n -> G e a t n", G=GROUPS, t=SLOTS, e=RUN)
+        c_view = c.rearrange("(G a l) -> a G l", G=GROUPS, l=C_ROW)
         zs_view = z_scales.bitcast(I32).rearrange("g q w -> q g w")
 
-        def load_x(i):
-            nc.sync.dma_start(out=x_raw[i][:], in_=x_view[i // 4, i // 2 % 2, i % 2])
+        def load_x(piece):
+            nc.sync.dma_start(out=x_raw[piece][:], in_=x_view[piece // 4, piece // 2 % 2, piece % 2])
 
         def load_z(G):
             nc.sync.dma_start(out=z_raw[G][:], in_=z_view[G])
 
         def load_alpha(G):
-            for e in range(4):
-                nc.sync.dma_start(out=a_raw[G][e:P:4, :, :], in_=a_view[G, e])
+            for e in range(RUN):
+                nc.sync.dma_start(out=a_raw[G][e:P:RUN, :, :], in_=a_view[G, e])
 
-        def load_z_scales(part, queue):
+        def load_z_scales(part):
             words = slice(P * part, P * (part + zs_groups[part]))
-            for Q in range(4):
-                queue.dma_start(out=zs_raw[part][32 * Q : 32 * Q + 4, :, :], in_=zs_view[4 * Q : 4 * Q + 4, :, words])
+            for s in range(4):
+                nc.sync.dma_start(out=zs_raw[part][s:P:32, :, :], in_=zs_view[s:16:4, :, words])
 
         nc.vector.memset(two[:], 2.0)
         nc.vector.memset(zs_raw[0][:], 0)
         nc.vector.memset(zs_raw[1][:], 0)
         make_identity(nc, ident[:])
-        for e in range(4):
-            nc.scalar.dma_start(out=c_raw[e:P:4, :, 0:13], in_=c_view[:, :, e : e + 13])
+        for e in range(RUN):
+            nc.scalar.dma_start(out=c_raw[e:P:RUN, :, 0:C_SPAN], in_=c_view[:, :, e : e + C_SPAN])
         nc.scalar.activation(out=ln_two[:], in_=two[:], func=ACT.Ln)
-        for i in range(HALF):
-            load_x(i)
-        load_z_scales(0, nc.sync)
+
+        for piece in range(PIECES // 2):
+            load_x(piece)
+        load_z_scales(0)
         load_z(0)
         load_alpha(0)
-        load_z_scales(1, nc.sync)
+        load_z_scales(1)
         load_z(1)
         load_z(2)
         load_alpha(1)
-        for i in range(HALF, TILES):
-            load_x(i)
+        for piece in range(PIECES // 2, PIECES):
+            load_x(piece)
         load_z(3)
         load_alpha(2)
         load_alpha(3)
@@ -119,9 +127,6 @@ def tile_landmark_kernel_ridge_s9_kernel(tc, x, z_words, z_scales, c, alpha, r, 
 
         c_bits = c_f32[:].rearrange("p G t -> p (G t)").bitcast(I32)
         sign = c_sign[:].bitcast(F32)
-
-        def widen_c():
-            nc.vector.tensor_copy(out=c_f32[:], in_=c_raw[:, :, 0:13:4])
 
         def split_c():
             nc.vector.tensor_scalar(out=c_mant[:], in0=c_bits, scalar1=0x007FFFFF, scalar2=0x3F800000,
@@ -137,23 +142,25 @@ def tile_landmark_kernel_ridge_s9_kernel(tc, x, z_words, z_scales, c, alpha, r, 
             nc.vector.tensor_scalar(out=zero_cap[:], in0=c_expo[:], scalar1=-0.5, scalar2=2.0**100,
                                     op0=ALU.add, op1=ALU.mult)
 
-        def transpose_x(i, engine):
-            bank = acc_ps.tile([P, 4, P], F32, name="acc")
-            for j in range(2):
-                words = x_raw[i][:, j, :].bitcast(F32)
-                for u in range(2):
-                    nc.tensor.transpose(bank[:, 2 * j + u, :], words[:, u:256:2], ident[:])
-            dst = x_grouped[i][:].bitcast(F32).rearrange("p (j m u) -> p j m u", j=2, u=2)
-            src = bank[:].rearrange("p (j u) m -> p j m u", u=2)
+        def move(engine, dst, src):
             if engine == "vector":
                 nc.vector.tensor_copy(out=dst, in_=src)
             else:
                 nc.scalar.copy(out=dst, in_=src)
 
-        def quantize_x(i):
-            cols = slice(256 * (i % 2), 256 * (i % 2 + 1))
-            nc.vector.quantize_mx(out=x_codes[i // 2][:, cols].bitcast(E4M3X4), scales=x_scales[i // 2][:, cols],
-                                  in_=x_grouped[i][:])
+        def transpose_x(piece, engine):
+            bank = acc_ps.tile([P, 4, P], F32, name="acc")
+            for j in range(2):
+                words = x_raw[piece][:, j, :].bitcast(F32)
+                for u in range(2):
+                    nc.tensor.transpose(bank[:, 2 * j + u, :], words[:, u : PASS // 2 : 2], ident[:])
+            move(engine, x_grouped[piece][:].bitcast(F32).rearrange("p (j m u) -> p j m u", j=2, u=2),
+                 bank[:].rearrange("p (j u) m -> p j m u", u=2))
+
+        def quantize_x(piece):
+            cols = slice(2 * P * (piece % 2), 2 * P * (piece % 2 + 1))
+            nc.vector.quantize_mx(out=x_codes[piece // 2][:, cols].bitcast(E4M3X4),
+                                  scales=x_scales[piece // 2][:, cols], in_=x_grouped[piece][:])
 
         def sort_z(G):
             nc.vector.tensor_copy(
@@ -162,22 +169,21 @@ def tile_landmark_kernel_ridge_s9_kernel(tc, x, z_words, z_scales, c, alpha, r, 
 
         def sort_z_scales(part):
             nc.vector.tensor_copy(
-                out=zs[part][:].bitcast(I32).rearrange("p (n t s a) -> p n s t a", t=SLOTS, s=8, a=4),
-                in_=zs_raw[part][:].rearrange("p g (G s a t) -> p (g G) s t a", s=8, a=4, t=SLOTS))
+                out=zs[part][:].bitcast(I32).rearrange("p (gG t hi lo) -> p gG hi t lo", t=SLOTS, hi=8, lo=4),
+                in_=zs_raw[part][:].rearrange("p g (G hi lo t) -> p (g G) hi t lo", hi=8, lo=4, t=SLOTS))
 
-        def interleave(engine, dst, src, lo, hi):
-            d = dst[:, lo:hi, :].rearrange("p (s i) t -> p s t i", i=4)
-            s = src[:, :, lo:hi].rearrange("p t (s i) -> p s t i", i=4)
-            if engine == "vector":
-                nc.vector.tensor_copy(out=d, in_=s)
-            else:
-                nc.scalar.copy(out=d, in_=s)
+        def interleave(engine, dst, src, first, end):
+            move(engine, dst[:, first:end, :].rearrange("p (quad n) t -> p quad t n", n=4),
+                 src[:, :, first:end].rearrange("p t (quad n) -> p quad t n", n=4))
 
         def sign_alpha(G):
             for t in range(SLOTS):
-                n = SLOTS * G + t
-                nc.vector.tensor_scalar(out=a_signed[G][:, t, :], in0=a_raw[G][:, t, :], scalar1=sign[:, n : n + 1],
-                                        scalar2=None, op0=ALU.mult)
+                col = SLOTS * G + t
+                nc.vector.tensor_scalar(out=a_signed[G][:, t, :], in0=a_raw[G][:, t, :],
+                                        scalar1=sign[:, col : col + 1], scalar2=None, op0=ALU.mult)
+
+        def group_alpha(G):
+            interleave("vector", a_grouped[G], a_signed[G], 0, R)
 
         def quantize_alpha(G):
             nc.vector.quantize_mx(out=a_codes[G][:].bitcast(E4M3X4), scales=a_scales[G][:],
@@ -186,71 +192,70 @@ def tile_landmark_kernel_ridge_s9_kernel(tc, x, z_words, z_scales, c, alpha, r, 
         h_slots = {}
         h_grouped = {}
 
-        def stage1(unit, share_of=None):
+        def first_product(unit, share_previous=False, x_pieces=()):
             half, G = divmod(unit, GROUPS)
-            h_slots[unit] = work.tile([P, SLOTS, 512], BF16, name="h_slots", align_bytes=64)
-            banks = [dots_ps.tile([P, 512], F32, name="dots") for t in range(SLOTS)]
+            part = min(G, 1)
+            h_slots[unit] = work.tile([P, SLOTS, HALF_COLS], BF16, name="h_slots", align_bytes=64)
+            banks = [dots_ps.tile([P, HALF_COLS], F32, name="dots") for t in range(SLOTS)]
             order = [(t, g) for t in range(SLOTS) for g in range(K_PASSES)]
             if unit == 0:
                 order = [(t, g) for g in range(K_PASSES) for t in range(SLOTS)]
             for t, g in order:
-                if unit == 2 and (t, g) == (1, 0):
-                    transpose_x(6, "scalar")
-                    transpose_x(7, "scalar")
-                w0 = 256 * (SLOTS * g + t)
-                part = min(G, 1)
-                s0 = 512 * (zs_groups[part] * g + G - part) + P * t
-                n = K_PASSES * half + g
-                nc.tensor.matmul_mx(out=banks[t][:], lhsT=z_codes[G][:, w0 : w0 + 256].bitcast(E2M1X4),
-                                    lhsT_scale=zs[part][:, s0 : s0 + P], rhs=x_codes[n][:].bitcast(E4M3X4),
-                                    rhs_scale=x_scales[n][:], start=(g == 0), stop=(g == K_PASSES - 1))
+                code_byte = 2 * P * (SLOTS * g + t)
+                scale_byte = PASS * (zs_groups[part] * g + G - part) + P * t
+                moving = K_PASSES * half + g
+                nc.tensor.matmul_mx(out=banks[t][:],
+                                    lhsT=z_codes[G][:, code_byte : code_byte + 2 * P].bitcast(E2M1X4),
+                                    lhsT_scale=zs[part][:, scale_byte : scale_byte + P],
+                                    rhs=x_codes[moving][:].bitcast(E4M3X4), rhs_scale=x_scales[moving][:],
+                                    start=(g == 0), stop=(g == K_PASSES - 1))
                 if g == K_PASSES - 1:
-                    n = SLOTS * G + t
+                    col = SLOTS * G + t
                     nc.scalar.activation(out=h_slots[unit][:, t, :], in_=banks[t][:], func=ACT.Exp,
-                                         bias=ln_c[:, n : n + 1])
-                    if t == 0 and share_of is not None:
-                        group_h(share_of, "scalar", split, 512)
+                                         bias=ln_c[:, col : col + 1])
+                    if t == 0:
+                        if share_previous:
+                            group_h(unit - 1, "scalar", VECTOR_COLS, HALF_COLS)
+                        for piece in x_pieces:
+                            transpose_x(piece, "scalar")
 
-        def group_h(unit, engine="vector", lo=0, hi=512):
+        def group_h(unit, engine="vector", first=0, end=HALF_COLS):
             if unit not in h_grouped:
-                h_grouped[unit] = work.tile([P, 512, SLOTS], BF16, name="h_grouped", align_bytes=64)
-            interleave(engine, h_grouped[unit], h_slots[unit], lo, hi)
+                h_grouped[unit] = work.tile([P, HALF_COLS, SLOTS], BF16, name="h_grouped", align_bytes=64)
+            interleave(engine, h_grouped[unit], h_slots[unit], first, end)
 
-        def quantize_h(unit, lo=0, hi=512):
-            nc.vector.quantize_mx(out=h_codes[unit][:, lo:hi].bitcast(E5M2X4), scales=h_scales[unit][:, lo:hi],
-                                  in_=h_grouped[unit][:, lo:hi, :].rearrange("p n t -> p (n t)"))
+        def quantize_h(unit, first=0, end=HALF_COLS):
+            nc.vector.quantize_mx(out=h_codes[unit][:, first:end].bitcast(E5M2X4),
+                                  scales=h_scales[unit][:, first:end],
+                                  in_=h_grouped[unit][:, first:end, :].rearrange("p n t -> p (n t)"))
 
         acc = {}
 
-        def stage2(i, groups):
-            cols = slice(P * (i % HALF), P * (i % HALF + 1))
+        def second_product(i, groups):
+            cols = slice(P * (i % HALF_TILES), P * (i % HALF_TILES + 1))
             for G in groups:
                 if G == 0:
                     acc[i] = acc_ps.tile([P, R], F32, name="acc")
-                unit = GROUPS * (i // HALF) + G
+                unit = GROUPS * (i // HALF_TILES) + G
                 nc.tensor.matmul_mx(out=acc[i][:], lhsT=h_codes[unit][:, cols].bitcast(E5M2X4),
                                     lhsT_scale=h_scales[unit][:, cols], rhs=a_codes[G][:].bitcast(E4M3X4),
                                     rhs_scale=a_scales[G][:], start=(G == 0), stop=(G == GROUPS - 1))
 
-        def stage2_first_half(G):
-            for i in range(HALF):
-                stage2(i, [G])
+        def second_product_first_half(G):
+            for i in range(HALF_TILES):
+                second_product(i, [G])
 
-        def finish(i, lo=0, hi=R):
-            nc.vector.scalar_tensor_tensor(out=y_sb[i][:, lo:hi], in0=acc[i][:, lo:hi], scalar=r_sb[:, i : i + 1],
-                                           in1=b_sb[:, lo:hi], op0=ALU.mult, op1=ALU.add)
-            nc.sync.dma_start(out=y_rows[i][:, lo:hi], in_=y_sb[i][:, lo:hi])
+        def finish(i, first=0, end=R):
+            nc.vector.scalar_tensor_tensor(out=y_sb[i][:, first:end], in0=acc[i][:, first:end],
+                                           scalar=r_sb[:, i : i + 1], in1=b_sb[:, first:end],
+                                           op0=ALU.mult, op1=ALU.add)
+            nc.sync.dma_start(out=y_rows[i][:, first:end], in_=y_sb[i][:, first:end])
 
-        split = 512 - SCALAR_COLS
-
-        def group_alpha(G, engine="vector", lo=0, hi=R):
-            interleave(engine, a_grouped[G], a_signed[G], lo, hi)
 
         transpose_x(0, "vector")
-        transpose_x(1, "scalar")
-        transpose_x(2, "scalar")
-        transpose_x(3, "scalar")
-        widen_c()
+        for piece in range(1, PIECES // 2):
+            transpose_x(piece, "scalar")
+        nc.vector.tensor_copy(out=c_f32[:], in_=c_raw[:, :, 0:C_SPAN:RUN])
         quantize_x(0)
         split_c()
         nc.scalar.activation(out=ln_mant[:], in_=c_mant[:].bitcast(F32), func=ACT.Ln)
@@ -262,75 +267,74 @@ def tile_landmark_kernel_ridge_s9_kernel(tc, x, z_words, z_scales, c, alpha, r, 
         nc.vector.tensor_tensor(out=ln_capped[:], in0=ln_expo[:], in1=zero_cap[:], op=ALU.min)
         quantize_x(3)
         nc.vector.tensor_tensor(out=ln_c[:], in0=ln_mant[:], in1=ln_capped[:], op=ALU.add)
+
         sign_alpha(0)
-        stage1(0)
+        first_product(0)
         sort_z_scales(1)
         sort_z(1)
-        group_alpha(0, "vector", 0, R - 0)
+        group_alpha(0)
         sort_z(2)
         quantize_alpha(0)
-        stage1(1)
+        first_product(1)
         sign_alpha(1)
         group_h(0)
         transpose_x(4, "scalar")
         transpose_x(5, "scalar")
         group_alpha(1)
         quantize_h(0)
-        group_h(1, "vector", 0, split)
+        group_h(1, "vector", 0, VECTOR_COLS)
         sort_z(3)
         quantize_alpha(1)
-        stage1(2, 1)
-        stage2_first_half(0)
-        sign_alpha(2)
-        quantize_h(1)
-        for i in range(HALF, TILES):
-            quantize_x(i)
-        group_alpha(2)
-        group_h(2, "vector", 0, split)
-        quantize_alpha(2)
-        stage1(3, 2)
-        stage2_first_half(1)
-        sign_alpha(3)
-        quantize_h(2)
-        group_alpha(3)
-        group_h(3, "vector", 0, split)
-        quantize_alpha(3)
-        stage1(4, 3)
-        stage2_first_half(2)
-        quantize_h(3)
-        group_h(4, "vector", 0, split)
-        stage1(5, 4)
-        stage2_first_half(3)
+
+        for unit in (2, 3, 4):
+            alpha_left = unit < GROUPS
+            first_product(unit, share_previous=True, x_pieces=(6, 7) if unit == 2 else ())
+            second_product_first_half(unit - 2)
+            if alpha_left:
+                sign_alpha(unit)
+            quantize_h(unit - 1)
+            if unit == 2:
+                for piece in range(PIECES // 2, PIECES):
+                    quantize_x(piece)
+            if alpha_left:
+                group_alpha(unit)
+            group_h(unit, "vector", 0, VECTOR_COLS)
+            if alpha_left:
+                quantize_alpha(unit)
+
+        first_product(5, share_previous=True)
+        second_product_first_half(3)
         quantize_h(4)
         finish(0)
         finish(1)
         group_h(5)
         finish(2)
-        stage1(6)
+        first_product(6)
         finish(3)
         quantize_h(5)
-        group_h(6, "vector", 0, 256)
-        group_h(6, "vector", 256, 512)
-        stage1(7)
-        quantize_h(6, 0, 256)
-        quantize_h(6, 256, 512)
-        group_h(7, "vector", 0, 128)
-        group_h(7, "scalar", 128, 256)
-        group_h(7, "scalar", 256, 384)
-        group_h(7, "scalar", 384, 512)
-        quantize_h(7, 0, 128)
-        quantize_h(7, 128, 256)
-        quantize_h(7, 256, 384)
+        halves = [(0, HALF_COLS // 2), (HALF_COLS // 2, HALF_COLS)]
+        for first, end in halves:
+            group_h(6, "vector", first, end)
+        first_product(7)
+        for first, end in halves:
+            quantize_h(6, first, end)
+
+        by_tile = [(first, first + P) for first in range(0, HALF_COLS, P)]
+        group_h(7, "vector", *by_tile[0])
+        for first, end in by_tile[1:]:
+            group_h(7, "scalar", first, end)
+        for first, end in by_tile[:3]:
+            quantize_h(7, first, end)
         for i in (4, 5, 6):
-            stage2(i, [0, 1])
+            second_product(i, [0, 1])
         for G in (2, 3):
-            stage2(4, [G])
-            stage2(5, [G])
+            second_product(4, [G])
+            second_product(5, [G])
         finish(4)
-        quantize_h(7, 384, 512)
+        quantize_h(7, *by_tile[3])
         finish(5)
-        stage2(6, [2, 3])
+        second_product(6, [2, 3])
         finish(6)
-        stage2(7, range(4))
+        second_product(7, range(GROUPS))
         finish(7, 0, R // 2)
         finish(7, R // 2, R)

from contextlib import ExitStack

import concourse.mybir as mybir
from concourse.masks import make_identity

M, K, N, R = 1024, 1024, 2048, 512
FLOPS = 2 * M * K * N + 2 * M * N * R

F32 = mybir.dt.float32
BF16 = mybir.dt.bfloat16
I32 = mybir.dt.int32
U32 = mybir.dt.uint32
U8 = mybir.dt.uint8
E4M3X4 = mybir.dt.float8_e4m3fn_x4
E5M2X4 = mybir.dt.float8_e5m2_x4
E2M1X4 = mybir.dt.float4_e2m1fn_x4
ALU = mybir.AluOpType
ACT = mybir.ActivationFunctionType

P = 128
SLOTS = 4
PASS = P * SLOTS
RUN = 4
K_PASSES = K // PASS
GROUPS = N // PASS
TILES = M // P
HALF_TILES = TILES // 2
HALF_COLS = HALF_TILES * P
PIECES = TILES
C_ROW = SLOTS * RUN
C_SPAN = C_ROW - RUN + 1
SCALAR_COLS = 176
VECTOR_COLS = HALF_COLS - SCALAR_COLS


def tile_landmark_kernel_ridge_s9_kernel(tc, x, z_words, z_scales, c, alpha, r, b, out):
    nc = tc.nc
    with ExitStack() as ctx:
        keep = ctx.enter_context(tc.tile_pool(name="keep", bufs=1))
        work = ctx.enter_context(tc.tile_pool(name="work", bufs=3))
        dots_ps = ctx.enter_context(tc.psum_pool(name="dots_ps", bufs=SLOTS))
        acc_ps = ctx.enter_context(tc.psum_pool(name="acc_ps", bufs=HALF_TILES))
        ctx.enter_context(tc.manual_schedule())

        def kept(name, count, shape, dtype):
            return [keep.tile(shape, dtype, name="%s%d" % (name, n), align_bytes=64) for n in range(count)]

        x_raw = kept("x_raw", PIECES, [P, 2, PASS], BF16)
        x_grouped = kept("x_grouped", PIECES, [P, 2 * P * SLOTS], BF16)
        x_codes = kept("x_codes", 2 * K_PASSES, [P, HALF_COLS], U32)
        x_scales = kept("x_scales", 2 * K_PASSES, [P, HALF_COLS], U8)
        z_raw = kept("z_raw", GROUPS, [P, K_PASSES, PASS // 2], I32)
        z_codes = kept("z_codes", GROUPS, [P, K_PASSES * SLOTS * 2 * P], U8)
        a_raw = kept("a_raw", GROUPS, [P, SLOTS, R], BF16)
        a_signed = kept("a_signed", GROUPS, [P, SLOTS, R], BF16)
        a_grouped = kept("a_grouped", GROUPS, [P, R, SLOTS], BF16)
        a_codes = kept("a_codes", GROUPS, [P, R], U32)
        a_scales = kept("a_scales", GROUPS, [P, R], U8)
        h_codes = kept("h_codes", 2 * GROUPS, [P, HALF_COLS], U32)
        h_scales = kept("h_scales", 2 * GROUPS, [P, HALF_COLS], U8)
        y_sb = kept("y_sb", TILES, [P, R], F32)
        zs_groups = (1, GROUPS - 1)
        zs_raw = [keep.tile([P, K_PASSES, P * n], I32, name="zs_raw%d" % n, align_bytes=64) for n in zs_groups]
        zs = [keep.tile([P, K_PASSES * PASS * n], U8, name="zs%d" % n, align_bytes=64) for n in zs_groups]
        ident = keep.tile([P, P], F32)
        c_raw = keep.tile([P, GROUPS, C_ROW], BF16)
        r_sb = keep.tile([P, TILES], BF16)
        b_sb = keep.tile([P, R], BF16)
        c_f32 = keep.tile([P, GROUPS, SLOTS], F32)
        c_expo = keep.tile([P, GROUPS * SLOTS], I32)
        c_mant = keep.tile([P, GROUPS * SLOTS], I32)
        c_sign = keep.tile([P, GROUPS * SLOTS], I32)
        ln_expo = keep.tile([P, GROUPS * SLOTS], F32)
        zero_cap = keep.tile([P, GROUPS * SLOTS], F32)
        ln_capped = keep.tile([P, GROUPS * SLOTS], F32)
        ln_mant = keep.tile([P, GROUPS * SLOTS], F32)
        ln_c = keep.tile([P, GROUPS * SLOTS], F32)
        two = keep.tile([P, 1], F32)
        ln_two = keep.tile([P, 1], F32)

        x_view = x.rearrange("(m h pair j) (g k) -> h g pair m j k", h=2, pair=2, j=2, g=K_PASSES)
        y_rows = out.rearrange("(m i) n -> i m n", i=TILES)
        z_view = z_words.bitcast(I32).rearrange("g p (G w) -> G p g w", G=GROUPS)
        a_view = alpha.rearrange("(G a t e) n -> G e a t n", G=GROUPS, t=SLOTS, e=RUN)
        c_view = c.rearrange("(G a l) -> a G l", G=GROUPS, l=C_ROW)
        zs_view = z_scales.bitcast(I32).rearrange("g q w -> q g w")

        def load_x(piece):
            nc.sync.dma_start(out=x_raw[piece][:], in_=x_view[piece // 4, piece // 2 % 2, piece % 2])

        def load_z(G):
            nc.sync.dma_start(out=z_raw[G][:], in_=z_view[G])

        def load_alpha(G):
            for e in range(RUN):
                nc.sync.dma_start(out=a_raw[G][e:P:RUN, :, :], in_=a_view[G, e])

        def load_z_scales(part):
            words = slice(P * part, P * (part + zs_groups[part]))
            for s in range(4):
                nc.sync.dma_start(out=zs_raw[part][s:P:32, :, :], in_=zs_view[s:16:4, :, words])

        nc.vector.memset(two[:], 2.0)
        nc.vector.memset(zs_raw[0][:], 0)
        nc.vector.memset(zs_raw[1][:], 0)
        make_identity(nc, ident[:])
        for e in range(RUN):
            nc.scalar.dma_start(out=c_raw[e:P:RUN, :, 0:C_SPAN], in_=c_view[:, :, e : e + C_SPAN])
        nc.scalar.activation(out=ln_two[:], in_=two[:], func=ACT.Ln)

        for piece in range(PIECES // 2):
            load_x(piece)
        load_z_scales(0)
        load_z(0)
        load_alpha(0)
        load_z_scales(1)
        load_z(1)
        load_z(2)
        load_alpha(1)
        for piece in range(PIECES // 2, PIECES):
            load_x(piece)
        load_z(3)
        load_alpha(2)
        load_alpha(3)
        nc.sync.dma_start(out=r_sb[:], in_=r.rearrange("(m i) -> m i", i=TILES))
        nc.sync.dma_start(out=b_sb[:], in_=b.partition_broadcast(P))

        c_bits = c_f32[:].rearrange("p G t -> p (G t)").bitcast(I32)
        sign = c_sign[:].bitcast(F32)

        def split_c():
            nc.vector.tensor_scalar(out=c_mant[:], in0=c_bits, scalar1=0x007FFFFF, scalar2=0x3F800000,
                                    op0=ALU.bitwise_and, op1=ALU.bitwise_or)
            nc.vector.tensor_scalar(out=c_expo[:], in0=c_bits, scalar1=23, scalar2=0xFF,
                                    op0=ALU.logical_shift_right, op1=ALU.bitwise_and)
            nc.vector.tensor_scalar(out=c_sign[:], in0=c_bits, scalar1=-0x80000000, scalar2=0x3F800000,
                                    op0=ALU.bitwise_and, op1=ALU.bitwise_or)

        def ln_exponent():
            nc.vector.tensor_scalar(out=ln_expo[:], in0=c_expo[:], scalar1=-127.0, scalar2=ln_two[:],
                                    op0=ALU.add, op1=ALU.mult)
            nc.vector.tensor_scalar(out=zero_cap[:], in0=c_expo[:], scalar1=-0.5, scalar2=2.0**100,
                                    op0=ALU.add, op1=ALU.mult)

        def move(engine, dst, src):
            if engine == "vector":
                nc.vector.tensor_copy(out=dst, in_=src)
            else:
                nc.scalar.copy(out=dst, in_=src)

        def transpose_x(piece, engine):
            bank = acc_ps.tile([P, 4, P], F32, name="acc")
            for j in range(2):
                words = x_raw[piece][:, j, :].bitcast(F32)
                for u in range(2):
                    nc.tensor.transpose(bank[:, 2 * j + u, :], words[:, u : PASS // 2 : 2], ident[:])
            move(engine, x_grouped[piece][:].bitcast(F32).rearrange("p (j m u) -> p j m u", j=2, u=2),
                 bank[:].rearrange("p (j u) m -> p j m u", u=2))

        def quantize_x(piece):
            cols = slice(2 * P * (piece % 2), 2 * P * (piece % 2 + 1))
            nc.vector.quantize_mx(out=x_codes[piece // 2][:, cols].bitcast(E4M3X4),
                                  scales=x_scales[piece // 2][:, cols], in_=x_grouped[piece][:])

        def sort_z(G):
            nc.vector.tensor_copy(
                out=z_codes[G][:].bitcast(I32).rearrange("p (g t a w) -> p g t a w", g=K_PASSES, t=SLOTS, w=2),
                in_=z_raw[G][:].rearrange("p g (a t w) -> p g t a w", t=SLOTS, w=2))

        def sort_z_scales(part):
            nc.vector.tensor_copy(
                out=zs[part][:].bitcast(I32).rearrange("p (gG t hi lo) -> p gG hi t lo", t=SLOTS, hi=8, lo=4),
                in_=zs_raw[part][:].rearrange("p g (G hi lo t) -> p (g G) hi t lo", hi=8, lo=4, t=SLOTS))

        def interleave(engine, dst, src, first, end):
            move(engine, dst[:, first:end, :].rearrange("p (quad n) t -> p quad t n", n=4),
                 src[:, :, first:end].rearrange("p t (quad n) -> p quad t n", n=4))

        def sign_alpha(G):
            for t in range(SLOTS):
                col = SLOTS * G + t
                nc.vector.tensor_scalar(out=a_signed[G][:, t, :], in0=a_raw[G][:, t, :],
                                        scalar1=sign[:, col : col + 1], scalar2=None, op0=ALU.mult)

        def group_alpha(G):
            interleave("vector", a_grouped[G], a_signed[G], 0, R)

        def quantize_alpha(G):
            nc.vector.quantize_mx(out=a_codes[G][:].bitcast(E4M3X4), scales=a_scales[G][:],
                                  in_=a_grouped[G][:].rearrange("p n t -> p (n t)"))

        h_slots = {}
        h_grouped = {}

        def first_product(unit, share_previous=False, x_pieces=()):
            half, G = divmod(unit, GROUPS)
            part = min(G, 1)
            h_slots[unit] = work.tile([P, SLOTS, HALF_COLS], BF16, name="h_slots", align_bytes=64)
            banks = [dots_ps.tile([P, HALF_COLS], F32, name="dots") for t in range(SLOTS)]
            order = [(t, g) for t in range(SLOTS) for g in range(K_PASSES)]
            if unit == 0:
                order = [(t, g) for g in range(K_PASSES) for t in range(SLOTS)]
            for t, g in order:
                code_byte = 2 * P * (SLOTS * g + t)
                scale_byte = PASS * (zs_groups[part] * g + G - part) + P * t
                moving = K_PASSES * half + g
                nc.tensor.matmul_mx(out=banks[t][:],
                                    lhsT=z_codes[G][:, code_byte : code_byte + 2 * P].bitcast(E2M1X4),
                                    lhsT_scale=zs[part][:, scale_byte : scale_byte + P],
                                    rhs=x_codes[moving][:].bitcast(E4M3X4), rhs_scale=x_scales[moving][:],
                                    start=(g == 0), stop=(g == K_PASSES - 1))
                if g == K_PASSES - 1:
                    col = SLOTS * G + t
                    nc.scalar.activation(out=h_slots[unit][:, t, :], in_=banks[t][:], func=ACT.Exp,
                                         bias=ln_c[:, col : col + 1])
                    if t == 0:
                        if share_previous:
                            group_h(unit - 1, "scalar", VECTOR_COLS, HALF_COLS)
                        for piece in x_pieces:
                            transpose_x(piece, "scalar")

        def group_h(unit, engine="vector", first=0, end=HALF_COLS):
            if unit not in h_grouped:
                h_grouped[unit] = work.tile([P, HALF_COLS, SLOTS], BF16, name="h_grouped", align_bytes=64)
            interleave(engine, h_grouped[unit], h_slots[unit], first, end)

        def quantize_h(unit, first=0, end=HALF_COLS):
            nc.vector.quantize_mx(out=h_codes[unit][:, first:end].bitcast(E5M2X4),
                                  scales=h_scales[unit][:, first:end],
                                  in_=h_grouped[unit][:, first:end, :].rearrange("p n t -> p (n t)"))

        acc = {}

        def second_product(i, groups):
            cols = slice(P * (i % HALF_TILES), P * (i % HALF_TILES + 1))
            for G in groups:
                if G == 0:
                    acc[i] = acc_ps.tile([P, R], F32, name="acc")
                unit = GROUPS * (i // HALF_TILES) + G
                nc.tensor.matmul_mx(out=acc[i][:], lhsT=h_codes[unit][:, cols].bitcast(E5M2X4),
                                    lhsT_scale=h_scales[unit][:, cols], rhs=a_codes[G][:].bitcast(E4M3X4),
                                    rhs_scale=a_scales[G][:], start=(G == 0), stop=(G == GROUPS - 1))

        def second_product_first_half(G):
            for i in range(HALF_TILES):
                second_product(i, [G])

        def finish(i, first=0, end=R):
            nc.vector.scalar_tensor_tensor(out=y_sb[i][:, first:end], in0=acc[i][:, first:end],
                                           scalar=r_sb[:, i : i + 1], in1=b_sb[:, first:end],
                                           op0=ALU.mult, op1=ALU.add)
            nc.sync.dma_start(out=y_rows[i][:, first:end], in_=y_sb[i][:, first:end])


        transpose_x(0, "vector")
        for piece in range(1, PIECES // 2):
            transpose_x(piece, "scalar")
        nc.vector.tensor_copy(out=c_f32[:], in_=c_raw[:, :, 0:C_SPAN:RUN])
        quantize_x(0)
        split_c()
        nc.scalar.activation(out=ln_mant[:], in_=c_mant[:].bitcast(F32), func=ACT.Ln)
        quantize_x(1)
        sort_z_scales(0)
        ln_exponent()
        sort_z(0)
        quantize_x(2)
        nc.vector.tensor_tensor(out=ln_capped[:], in0=ln_expo[:], in1=zero_cap[:], op=ALU.min)
        quantize_x(3)
        nc.vector.tensor_tensor(out=ln_c[:], in0=ln_mant[:], in1=ln_capped[:], op=ALU.add)

        sign_alpha(0)
        first_product(0)
        sort_z_scales(1)
        sort_z(1)
        group_alpha(0)
        sort_z(2)
        quantize_alpha(0)
        first_product(1)
        sign_alpha(1)
        group_h(0)
        transpose_x(4, "scalar")
        transpose_x(5, "scalar")
        group_alpha(1)
        quantize_h(0)
        group_h(1, "vector", 0, VECTOR_COLS)
        sort_z(3)
        quantize_alpha(1)

        for unit in (2, 3, 4):
            alpha_left = unit < GROUPS
            first_product(unit, share_previous=True, x_pieces=(6, 7) if unit == 2 else ())
            second_product_first_half(unit - 2)
            if alpha_left:
                sign_alpha(unit)
            quantize_h(unit - 1)
            if unit == 2:
                for piece in range(PIECES // 2, PIECES):
                    quantize_x(piece)
            if alpha_left:
                group_alpha(unit)
            group_h(unit, "vector", 0, VECTOR_COLS)
            if alpha_left:
                quantize_alpha(unit)

        first_product(5, share_previous=True)
        second_product_first_half(3)
        quantize_h(4)
        finish(0)
        finish(1)
        group_h(5)
        finish(2)
        first_product(6)
        finish(3)
        quantize_h(5)
        halves = [(0, HALF_COLS // 2), (HALF_COLS // 2, HALF_COLS)]
        for first, end in halves:
            group_h(6, "vector", first, end)
        first_product(7)
        for first, end in halves:
            quantize_h(6, first, end)

        by_tile = [(first, first + P) for first in range(0, HALF_COLS, P)]
        group_h(7, "vector", *by_tile[0])
        for first, end in by_tile[1:]:
            group_h(7, "scalar", first, end)
        for first, end in by_tile[:3]:
            quantize_h(7, first, end)
        for i in (4, 5, 6):
            second_product(i, [0, 1])
        for G in (2, 3):
            second_product(4, [G])
            second_product(5, [G])
        finish(4)
        quantize_h(7, *by_tile[3])
        finish(5)
        second_product(6, [2, 3])
        finish(6)
        second_product(7, range(GROUPS))
        finish(7, 0, R // 2)
        finish(7, R // 2, R)
